import numpy as np
import ml_dtypes


def mxq(x, axis, fmt="e4m3"):
    dtype, down = {"e4m3": (ml_dtypes.float8_e4m3fn, 7), "e5m2": (ml_dtypes.float8_e5m2, 14)}[fmt]
    v = np.moveaxis(np.asarray(x, np.float32).astype(ml_dtypes.bfloat16).astype(np.float64), axis, -1)
    blocks = v.reshape(v.shape[:-1] + (-1, 32))
    amax = np.abs(blocks).max(-1, keepdims=True)
    byte = np.maximum(np.where(amax > 0, np.frexp(amax)[1] - 1 + 127, 0) - down, 1)
    scale = np.exp2(byte - 127.0)
    codes = (blocks / scale).astype(np.float32).astype(dtype).astype(np.float64)
    return np.moveaxis((codes * scale).reshape(v.shape), -1, axis)


WIDE = False


def mx_kscale(k):
    if not WIDE:
        return np.ones(k)
    levels = np.array([10, -10, 5, -5, 0])
    if k % 512:
        return np.exp2(np.random.permutation(np.resize(levels, k // 32))).repeat(32)
    a = np.empty((k // 512, 16))
    for p in range(k // 512):
        a[p, :8] = np.random.permutation(np.resize(levels, 8))
        for g in range(8):
            far = levels[np.abs(levels - a[p, g]) >= 10]
            a[p, g + 8] = far[np.random.randint(len(far))]
    return np.exp2(a.ravel()).repeat(32)


def f64(x):
    return np.asarray(x).astype(np.float64)


def striped(idx):
    return np.tile(idx.reshape(-1, 16).T, (8, 1)).astype(np.uint16)


def unstriped(offs):
    return offs[:16].T.reshape(-1).astype(np.int64)


K, T, D, S, V, N = 1024, 1024, 3, 768, 256, 256


def setup_inputs():
    n = np.random.standard_normal
    s = mx_kscale(K)[:, None]
    return {
        "xT": (n((K, T)) * s / np.sqrt(D)).astype(ml_dtypes.bfloat16).astype(np.float32),
        "w": (n((K, N)) / np.sqrt(K) / s).astype(np.float32),
        "offs": striped(np.concatenate([np.random.permutation(T)[:V] for _ in range(D)])),
    }


def reference(xT, w, offs):
    idx = unstriped(offs)
    x = sum(f64(xT)[:, idx[d * V:(d + 1) * V]] for d in range(D))
    return mxq(f64(w), 0, "e4m3").T @ mxq(x, 0, "e4m3")

@@ -1,0 +1,164 @@
+from contextlib import ExitStack
+
+import concourse.mybir as mybir
+
+K, T, D, V, N = 1024, 1024, 3, 256, 256
+FLOPS = 2 * K * N * V
+
+F32 = mybir.dt.float32
+BF16 = mybir.dt.bfloat16
+U32 = mybir.dt.uint32
+U16 = mybir.dt.uint16
+U8 = mybir.dt.uint8
+FP8X4 = mybir.dt.float8_e4m3fn_x4
+ADD = mybir.AluOpType.add
+
+P = 128
+PACK = 4
+PASSES = K // (P * PACK)
+PAIRS = PACK // 2
+HALF = V // 2
+COLS = V // 16
+
+CHUNKS = [
+    [(0, 768, "vector"), (768, 1024, "vector")],
+    [(0, 384, "scalar"), (384, 768, "scalar"), (768, 1024, "vector")],
+    [(0, 512, "scalar"), (512, 1024, "scalar")],
+    [(0, 512, "scalar"), (512, 1024, "scalar")],
+]
+
+
+def tile_picked_hash_lin_none_sub_l_kernel(tc, xT, w, offs, out):
+    nc = tc.nc
+    x_rows = xT.rearrange("(g p j) t -> g p j t", p=P, j=PACK)
+    w_rows = w.rearrange("(g p j) n -> g p j n", p=P, j=PACK)
+    out_rows = out.rearrange("(b p) v -> p b v", p=P)
+
+    with ExitStack() as ctx:
+        keep = ctx.enter_context(tc.tile_pool(name="keep", bufs=1))
+        psum = ctx.enter_context(tc.psum_pool(name="psum", bufs=1))
+
+        warm_in = keep.tile([P, 8], F32, name="warm_in")
+        warm_out = keep.tile([P, 8], BF16, name="warm_out")
+        nc.vector.memset(warm_in[:], 0.0)
+        nc.scalar.copy(warm_out[:], warm_in[:])
+
+        offsets = keep.tile([P, D * COLS], U16, name="offsets")
+
+        raw = {}
+        for q in range(PASSES * PAIRS):
+            g, u = divmod(q, PAIRS)
+            for c, (lo, hi, engine) in enumerate(CHUNKS[q]):
+                raw[q, c] = keep.tile([P, 2, hi - lo], F32, name="raw%d_%d" % (q, c))
+                nc.sync.dma_start(raw[q, c][:], x_rows[g, :, 2 * u : 2 * u + 2, lo:hi])
+                if q == 0 and c == 0:
+                    nc.sync.dma_start(offsets[:], offs)
+        w_raw = []
+        for g in range(PASSES):
+            w_raw.append(keep.tile([P, PACK, N], F32, name="w_raw%d" % g))
+            nc.sync.dma_start(w_raw[g][:], w_rows[g])
+
+        table = [keep.tile([P, T, 2], BF16, name="table%d" % q) for q in range(PASSES * PAIRS)]
+        picked = [keep.tile([P, PAIRS, D, V, 2], BF16, name="picked%d" % g) for g in range(PASSES)]
+        partial = [keep.tile([P, PAIRS, V, 2], F32, name="partial%d" % g) for g in range(PASSES)]
+        x_bf = [keep.tile([P, V, PAIRS, 2], BF16, name="x_bf%d" % g, align_bytes=64) for g in range(PASSES)]
+        w_bf = [keep.tile([P, N, PACK], BF16, name="w_bf%d" % g, align_bytes=64) for g in range(PASSES)]
+        x_codes = [keep.tile([P, V], U32, name="x_codes%d" % g, align_bytes=64) for g in range(PASSES)]
+        x_scales = [keep.tile([P, V], U8, name="x_scales%d" % g, align_bytes=64) for g in range(PASSES)]
+        w_codes = [keep.tile([P, N], U32, name="w_codes%d" % g, align_bytes=64) for g in range(PASSES)]
+        w_scales = [keep.tile([P, N], U8, name="w_scales%d" % g, align_bytes=64) for g in range(PASSES)]
+        acc = {(h, b): psum.tile([P, HALF], F32, name="acc%d_%d" % (h, b)) for h in range(2) for b in range(2)}
+        result = [keep.tile([P, 2, HALF], F32, name="result%d" % h) for h in range(2)]
+
+        def pair_up(q):
+            for c, (lo, hi, engine) in enumerate(CHUNKS[q]):
+                source = raw[q, c][:].rearrange("p e t -> p t e")
+                if engine == "vector":
+                    nc.vector.tensor_copy(table[q][:, lo:hi, :], source)
+                else:
+                    nc.scalar.copy(table[q][:, lo:hi, :], source)
+
+        def gather(q, d_lo, d_hi):
+            g, u = divmod(q, PAIRS)
+            window = table[q][:].rearrange("p t e -> p (t e)").bitcast(U32)
+            words = picked[g][:, u, d_lo:d_hi].rearrange("p d v e -> p (d v e)").bitcast(U32)
+            nc.vector.tensor_copy(words, window.indirect(offsets[:, d_lo * COLS : d_hi * COLS]))
+
+        def add_first(q):
+            g, u = divmod(q, PAIRS)
+            nc.vector.tensor_tensor(partial[g][:, u], picked[g][:, u, 0], picked[g][:, u, 1], ADD)
+
+        def add_last(g, lo, hi):
+            nc.vector.tensor_tensor(
+                x_bf[g][:, lo:hi],
+                partial[g][:, :, lo:hi].rearrange("p u v e -> p v u e"),
+                picked[g][:, :, 2, lo:hi].rearrange("p u v e -> p v u e"),
+                ADD,
+            )
+
+        def quantize_x(g, lo, hi):
+            nc.vector.quantize_mx(
+                out=x_codes[g][:, lo:hi].bitcast(FP8X4),
+                scales=x_scales[g][:, lo:hi],
+                in_=x_bf[g][:, lo:hi].rearrange("p v u e -> p (v u e)"),
+            )
+
+        def interleave_w(g):
+            nc.scalar.copy(w_bf[g][:], w_raw[g][:].rearrange("p j n -> p n j"))
+
+        def quantize_w(g):
+            nc.vector.quantize_mx(
+                out=w_codes[g][:].bitcast(FP8X4),
+                scales=w_scales[g][:],
+                in_=w_bf[g][:].rearrange("p n j -> p (n j)"),
+            )
+
+        def multiply(g, h):
+            ids = slice(h * HALF, (h + 1) * HALF)
+            for b in range(2):
+                rows = slice(b * P, (b + 1) * P)
+                nc.tensor.matmul_mx(
+                    out=acc[h, b][:],
+                    lhsT=w_codes[g][:, rows].bitcast(FP8X4),
+                    lhsT_scale=w_scales[g][:, rows],
+                    rhs=x_codes[g][:, ids].bitcast(FP8X4),
+                    rhs_scale=x_scales[g][:, ids],
+                    start=(g == 0),
+                    stop=(g == PASSES - 1),
+                )
+
+        pair_up(0)
+        gather(0, 0, 2)
+        gather(0, 2, 3)
+        add_first(0)
+        pair_up(1)
+        gather(1, 0, 2)
+        gather(1, 2, 3)
+        add_first(1)
+        pair_up(2)
+        add_last(0, 0, V)
+        gather(2, 0, 2)
+        quantize_x(0, 0, V)
+        gather(2, 2, 3)
+        add_first(2)
+        pair_up(3)
+        gather(3, 0, 2)
+        gather(3, 2, 3)
+        interleave_w(0)
+        quantize_w(0)
+        multiply(0, 0)
+        multiply(0, 1)
+        add_first(3)
+        interleave_w(1)
+        quantize_w(1)
+        add_last(1, 0, HALF)
+        add_last(1, HALF, V)
+        for h in range(2):
+            quantize_x(1, h * HALF, (h + 1) * HALF)
+            multiply(1, h)
+        nc.scalar.copy(result[0][:, 0], acc[0, 0][:])
+        nc.scalar.copy(result[0][:, 1], acc[0, 1][:])
+        nc.sync.dma_start(out_rows[:, :, 0:HALF], result[0][:])
+        nc.vector.tensor_copy(result[1][:, 0], acc[1, 0][:])
+        nc.scalar.copy(result[1][:, 1], acc[1, 1][:])
+        nc.sync.dma_start(out_rows[:, :, HALF:V], result[1][:])

@@ -21,11 +21,12 @@ HALF = V // 2
 COLS = V // 16
 
 CHUNKS = [
-    [(0, 768, "vector"), (768, 1024, "vector")],
-    [(0, 384, "scalar"), (384, 768, "scalar"), (768, 1024, "vector")],
+    [(0, 512, "scalar"), (512, 1024, "both")],
+    [(0, 384, "scalar"), (384, 768, "scalar"), (768, 1024, "scalar")],
     [(0, 512, "scalar"), (512, 1024, "scalar")],
     [(0, 512, "scalar"), (512, 1024, "scalar")],
 ]
+SPLIT = 352
 
 
 def tile_picked_hash_lin_none_sub_l_kernel(tc, xT, w, offs, out):
@@ -75,6 +76,9 @@ def tile_picked_hash_lin_none_sub_l_kernel(tc, xT, w, offs, out):
                 source = raw[q, c][:].rearrange("p e t -> p t e")
                 if engine == "vector":
                     nc.vector.tensor_copy(table[q][:, lo:hi, :], source)
+                elif engine == "both":
+                    nc.vector.tensor_copy(table[q][:, lo : lo + SPLIT, :], source[:, 0:SPLIT])
+                    nc.scalar.copy(table[q][:, lo + SPLIT : hi, :], source[:, SPLIT : hi - lo])
                 else:
                     nc.scalar.copy(table[q][:, lo:hi, :], source)
 
@@ -84,12 +88,12 @@ def tile_picked_hash_lin_none_sub_l_kernel(tc, xT, w, offs, out):
             words = picked[g][:, u, d_lo:d_hi].rearrange("p d v e -> p (d v e)").bitcast(U32)
             nc.vector.tensor_copy(words, window.indirect(offsets[:, d_lo * COLS : d_hi * COLS]))
 
-        def add_first(q):
+        def add_first(q, engine):
             g, u = divmod(q, PAIRS)
-            nc.vector.tensor_tensor(partial[g][:, u], picked[g][:, u, 0], picked[g][:, u, 1], ADD)
+            engine.tensor_tensor(partial[g][:, u], picked[g][:, u, 0], picked[g][:, u, 1], ADD)
 
-        def add_last(g, lo, hi):
-            nc.vector.tensor_tensor(
+        def add_last(g, lo, hi, engine):
+            engine.tensor_tensor(
                 x_bf[g][:, lo:hi],
                 partial[g][:, :, lo:hi].rearrange("p u v e -> p v u e"),
                 picked[g][:, :, 2, lo:hi].rearrange("p u v e -> p v u e"),
@@ -129,30 +133,31 @@ def tile_picked_hash_lin_none_sub_l_kernel(tc, xT, w, offs, out):
 
         pair_up(0)
         gather(0, 0, 2)
+        add_first(0, nc.gpsimd)
         gather(0, 2, 3)
-        add_first(0)
         pair_up(1)
         gather(1, 0, 2)
+        add_first(1, nc.gpsimd)
         gather(1, 2, 3)
-        add_first(1)
+        add_last(0, 0, HALF, nc.gpsimd)
+        add_last(0, HALF, V, nc.gpsimd)
         pair_up(2)
-        add_last(0, 0, V)
         gather(2, 0, 2)
-        quantize_x(0, 0, V)
+        add_first(2, nc.gpsimd)
         gather(2, 2, 3)
-        add_first(2)
         pair_up(3)
         gather(3, 0, 2)
         gather(3, 2, 3)
+        add_first(3, nc.vector)
+        quantize_x(0, 0, V)
         interleave_w(0)
+        add_last(1, 0, HALF, nc.vector)
+        add_last(1, HALF, V, nc.vector)
         quantize_w(0)
         multiply(0, 0)
         multiply(0, 1)
-        add_first(3)
         interleave_w(1)
         quantize_w(1)
-        add_last(1, 0, HALF)
-        add_last(1, HALF, V)
         for h in range(2):
             quantize_x(1, h * HALF, (h + 1) * HALF)
             multiply(1, h)

@@ -60,14 +60,23 @@ def tile_picked_hash_lin_none_sub_l_kernel(tc, xT, w, offs, out):
             nc.sync.dma_start(w_raw[g][:], w_rows[g])
 
         table = [keep.tile([P, T, 2], BF16, name="table%d" % q) for q in range(PASSES * PAIRS)]
-        picked = [keep.tile([P, PAIRS, D, V, 2], BF16, name="picked%d" % g) for g in range(PASSES)]
+        picked = [keep.tile([P, PAIRS, D, V + 8, 2], BF16, name="picked%d" % g) for g in range(PASSES)]
         partial = [keep.tile([P, PAIRS, V, 2], F32, name="partial%d" % g) for g in range(PASSES)]
-        x_bf = [keep.tile([P, V, PAIRS, 2], BF16, name="x_bf%d" % g, align_bytes=64) for g in range(PASSES)]
-        w_bf = [keep.tile([P, N, PACK], BF16, name="w_bf%d" % g, align_bytes=64) for g in range(PASSES)]
-        x_codes = [keep.tile([P, V], U32, name="x_codes%d" % g, align_bytes=64) for g in range(PASSES)]
-        x_scales = [keep.tile([P, V], U8, name="x_scales%d" % g, align_bytes=64) for g in range(PASSES)]
-        w_codes = [keep.tile([P, N], U32, name="w_codes%d" % g, align_bytes=64) for g in range(PASSES)]
-        w_scales = [keep.tile([P, N], U8, name="w_scales%d" % g, align_bytes=64) for g in range(PASSES)]
+        both_bf = keep.tile([P, 2, V * PACK], BF16, name="both_bf", align_bytes=64)
+        both_codes = keep.tile([P, 2, V], U32, name="both_codes", align_bytes=64)
+        both_scales = keep.tile([P, 2, V], U8, name="both_scales", align_bytes=64)
+        x_bf1 = keep.tile([P, V * PACK], BF16, name="x_bf1", align_bytes=64)
+        w_bf1 = keep.tile([P, N * PACK], BF16, name="w_bf1", align_bytes=64)
+        x_codes1 = keep.tile([P, V], U32, name="x_codes1", align_bytes=64)
+        x_scales1 = keep.tile([P, V], U8, name="x_scales1", align_bytes=64)
+        w_codes1 = keep.tile([P, N], U32, name="w_codes1", align_bytes=64)
+        w_scales1 = keep.tile([P, N], U8, name="w_scales1", align_bytes=64)
+        x_bf = [t.rearrange("p (v u e) -> p v u e", u=PAIRS, e=2) for t in (both_bf[:, 0], x_bf1[:])]
+        w_bf = [t.rearrange("p (n j) -> p n j", j=PACK) for t in (both_bf[:, 1], w_bf1[:])]
+        x_codes = [both_codes[:, 0], x_codes1[:]]
+        x_scales = [both_scales[:, 0], x_scales1[:]]
+        w_codes = [both_codes[:, 1], w_codes1[:]]
+        w_scales = [both_scales[:, 1], w_scales1[:]]
         acc = {(h, b): psum.tile([P, HALF], F32, name="acc%d_%d" % (h, b)) for h in range(2) for b in range(2)}
         result = [keep.tile([P, 2, HALF], F32, name="result%d" % h) for h in range(2)]
 
@@ -85,12 +94,12 @@ def tile_picked_hash_lin_none_sub_l_kernel(tc, xT, w, offs, out):
         def gather(q, d_lo, d_hi):
             g, u = divmod(q, PAIRS)
             window = table[q][:].rearrange("p t e -> p (t e)").bitcast(U32)
-            words = picked[g][:, u, d_lo:d_hi].rearrange("p d v e -> p (d v e)").bitcast(U32)
+            words = picked[g][:, u].rearrange("p d v e -> p d (v e)").bitcast(U32)[:, d_lo:d_hi, 0:V]
             nc.vector.tensor_copy(words, window.indirect(offsets[:, d_lo * COLS : d_hi * COLS]))
 
         def add_first(q, engine):
             g, u = divmod(q, PAIRS)
-            engine.tensor_tensor(partial[g][:, u], picked[g][:, u, 0], picked[g][:, u, 1], ADD)
+            engine.tensor_tensor(partial[g][:, u], picked[g][:, u, 0, 0:V], picked[g][:, u, 1, 0:V], ADD)
 
         def add_last(g, lo, hi, engine):
             engine.tensor_tensor(
@@ -108,13 +117,13 @@ def tile_picked_hash_lin_none_sub_l_kernel(tc, xT, w, offs, out):
             )
 
         def interleave_w(g):
-            nc.scalar.copy(w_bf[g][:], w_raw[g][:].rearrange("p j n -> p n j"))
+            nc.scalar.copy(w_bf[g], w_raw[g][:].rearrange("p j n -> p n j"))
 
         def quantize_w(g):
             nc.vector.quantize_mx(
-                out=w_codes[g][:].bitcast(FP8X4),
-                scales=w_scales[g][:],
-                in_=w_bf[g][:].rearrange("p n j -> p (n j)"),
+                out=w_codes[g].bitcast(FP8X4),
+                scales=w_scales[g],
+                in_=w_bf[g].rearrange("p n j -> p (n j)"),
             )
 
         def multiply(g, h):
@@ -132,32 +141,31 @@ def tile_picked_hash_lin_none_sub_l_kernel(tc, xT, w, offs, out):
                 )
 
         pair_up(0)
-        gather(0, 0, 2)
-        add_first(0, nc.gpsimd)
-        gather(0, 2, 3)
+        gather(0, 0, 3)
+        add_first(0, nc.vector)
         pair_up(1)
-        gather(1, 0, 2)
-        add_first(1, nc.gpsimd)
-        gather(1, 2, 3)
+        gather(1, 0, 3)
+        add_first(1, nc.vector)
         add_last(0, 0, HALF, nc.gpsimd)
         add_last(0, HALF, V, nc.gpsimd)
         pair_up(2)
-        gather(2, 0, 2)
+        gather(2, 0, 3)
         add_first(2, nc.gpsimd)
-        gather(2, 2, 3)
         pair_up(3)
-        gather(3, 0, 2)
-        gather(3, 2, 3)
-        add_first(3, nc.vector)
-        quantize_x(0, 0, V)
+        gather(3, 0, 3)
         interleave_w(0)
-        add_last(1, 0, HALF, nc.vector)
-        add_last(1, HALF, V, nc.vector)
-        quantize_w(0)
+        nc.vector.quantize_mx(
+            out=both_codes[:].rearrange("p s v -> p (s v)").bitcast(FP8X4),
+            scales=both_scales[:].rearrange("p s v -> p (s v)"),
+            in_=both_bf[:].rearrange("p s c -> p (s c)"),
+        )
         multiply(0, 0)
         multiply(0, 1)
+        add_first(3, nc.vector)
         interleave_w(1)
         quantize_w(1)
+        add_last(1, 0, HALF, nc.vector)
+        add_last(1, HALF, V, nc.vector)
         for h in range(2):
             quantize_x(1, h * HALF, (h + 1) * HALF)
             multiply(1, h)

@@ -18,15 +18,11 @@ PACK = 4
 PASSES = K // (P * PACK)
 PAIRS = PACK // 2
 HALF = V // 2
-COLS = V // 16
-
-CHUNKS = [
-    [(0, 512, "scalar"), (512, 1024, "both")],
-    [(0, 384, "scalar"), (384, 768, "scalar"), (768, 1024, "scalar")],
-    [(0, 512, "scalar"), (512, 1024, "scalar")],
-    [(0, 512, "scalar"), (512, 1024, "scalar")],
-]
-SPLIT = 352
+RUNS = 2 * D
+RUN_COLS = HALF // 16
+PAD = 8
+CHUNK = T // 2
+VECTOR_SHARE = [352,223,223,223]
 
 
 def tile_picked_hash_lin_none_sub_l_kernel(tc, xT, w, offs, out):
@@ -44,134 +40,135 @@ def tile_picked_hash_lin_none_sub_l_kernel(tc, xT, w, offs, out):
         nc.vector.memset(warm_in[:], 0.0)
         nc.scalar.copy(warm_out[:], warm_in[:])
 
-        offsets = keep.tile([P, D * COLS], U16, name="offsets")
-
+        offsets = keep.tile([P, RUNS * RUN_COLS], U16, name="offsets")
         raw = {}
         for q in range(PASSES * PAIRS):
             g, u = divmod(q, PAIRS)
-            for c, (lo, hi, engine) in enumerate(CHUNKS[q]):
-                raw[q, c] = keep.tile([P, 2, hi - lo], F32, name="raw%d_%d" % (q, c))
-                nc.sync.dma_start(raw[q, c][:], x_rows[g, :, 2 * u : 2 * u + 2, lo:hi])
-                if q == 0 and c == 0:
-                    nc.sync.dma_start(offsets[:], offs)
+            for c in range(2):
+                raw[q, c] = keep.tile([P, 2, CHUNK], F32, name="raw%d_%d" % (q, c))
+                nc.sync.dma_start(raw[q, c][:], x_rows[g, :, 2 * u : 2 * u + 2, c * CHUNK : (c + 1) * CHUNK])
+            if q == 0:
+                nc.sync.dma_start(offsets[:], offs)
         w_raw = []
         for g in range(PASSES):
-            w_raw.append(keep.tile([P, PACK, N], F32, name="w_raw%d" % g))
+            w_raw.append(keep.tile([P, PACK, N], F32, name="w_raw%d" % g, align_bytes=64))
             nc.sync.dma_start(w_raw[g][:], w_rows[g])
 
         table = [keep.tile([P, T, 2], BF16, name="table%d" % q) for q in range(PASSES * PAIRS)]
-        picked = [keep.tile([P, PAIRS, D, V + 8, 2], BF16, name="picked%d" % g) for g in range(PASSES)]
-        partial = [keep.tile([P, PAIRS, V, 2], F32, name="partial%d" % g) for g in range(PASSES)]
+        picked = [
+            keep.tile([P, PAIRS, RUNS, HALF + PAD, 2], BF16, name="picked%d" % g, align_bytes=64)
+            for g in range(PASSES)
+        ]
+        partial = [keep.tile([P, PAIRS, 2, HALF, 2], F32, name="partial%d" % g) for g in range(PASSES)]
         both_bf = keep.tile([P, 2, V * PACK], BF16, name="both_bf", align_bytes=64)
         both_codes = keep.tile([P, 2, V], U32, name="both_codes", align_bytes=64)
         both_scales = keep.tile([P, 2, V], U8, name="both_scales", align_bytes=64)
-        x_bf1 = keep.tile([P, V * PACK], BF16, name="x_bf1", align_bytes=64)
         w_bf1 = keep.tile([P, N * PACK], BF16, name="w_bf1", align_bytes=64)
-        x_codes1 = keep.tile([P, V], U32, name="x_codes1", align_bytes=64)
-        x_scales1 = keep.tile([P, V], U8, name="x_scales1", align_bytes=64)
         w_codes1 = keep.tile([P, N], U32, name="w_codes1", align_bytes=64)
+        x_scales1 = keep.tile([P, V], U8, name="x_scales1", align_bytes=64)
         w_scales1 = keep.tile([P, N], U8, name="w_scales1", align_bytes=64)
-        x_bf = [t.rearrange("p (v u e) -> p v u e", u=PAIRS, e=2) for t in (both_bf[:, 0], x_bf1[:])]
-        w_bf = [t.rearrange("p (n j) -> p n j", j=PACK) for t in (both_bf[:, 1], w_bf1[:])]
-        x_codes = [both_codes[:, 0], x_codes1[:]]
-        x_scales = [both_scales[:, 0], x_scales1[:]]
-        w_codes = [both_codes[:, 1], w_codes1[:]]
-        w_scales = [both_scales[:, 1], w_scales1[:]]
+        w_bf = [both_bf[:, 1], w_bf1[:]]
         acc = {(h, b): psum.tile([P, HALF], F32, name="acc%d_%d" % (h, b)) for h in range(2) for b in range(2)}
         result = [keep.tile([P, 2, HALF], F32, name="result%d" % h) for h in range(2)]
 
         def pair_up(q):
-            for c, (lo, hi, engine) in enumerate(CHUNKS[q]):
-                source = raw[q, c][:].rearrange("p e t -> p t e")
-                if engine == "vector":
-                    nc.vector.tensor_copy(table[q][:, lo:hi, :], source)
-                elif engine == "both":
-                    nc.vector.tensor_copy(table[q][:, lo : lo + SPLIT, :], source[:, 0:SPLIT])
-                    nc.scalar.copy(table[q][:, lo + SPLIT : hi, :], source[:, SPLIT : hi - lo])
-                else:
-                    nc.scalar.copy(table[q][:, lo:hi, :], source)
+            share = VECTOR_SHARE[q]
+            first = raw[q, 0][:].rearrange("p e t -> p t e")
+            second = raw[q, 1][:].rearrange("p e t -> p t e")
+            nc.scalar.copy(table[q][:, 0:CHUNK, :], first)
+            nc.scalar.copy(table[q][:, CHUNK : T - share, :], second[:, 0 : CHUNK - share])
+            nc.vector.tensor_copy(table[q][:, T - share : T, :], second[:, CHUNK - share : CHUNK])
 
-        def gather(q, d_lo, d_hi):
+        def gather(q, part):
             g, u = divmod(q, PAIRS)
             window = table[q][:].rearrange("p t e -> p (t e)").bitcast(U32)
-            words = picked[g][:, u].rearrange("p d v e -> p d (v e)").bitcast(U32)[:, d_lo:d_hi, 0:V]
-            nc.vector.tensor_copy(words, window.indirect(offsets[:, d_lo * COLS : d_hi * COLS]))
+            words = picked[g][:, u].rearrange("p r v e -> p r (v e)").bitcast(U32)
+            nc.vector.tensor_copy(
+                words[:, D * part : D * (part + 1), 0:HALF],
+                window.indirect(offsets[:, D * part * RUN_COLS : D * (part + 1) * RUN_COLS]),
+            )
 
-        def add_first(q, engine):
+        def add_first(q, h_lo, h_hi, engine):
             g, u = divmod(q, PAIRS)
-            engine.tensor_tensor(partial[g][:, u], picked[g][:, u, 0, 0:V], picked[g][:, u, 1, 0:V], ADD)
-
-        def add_last(g, lo, hi, engine):
             engine.tensor_tensor(
-                x_bf[g][:, lo:hi],
-                partial[g][:, :, lo:hi].rearrange("p u v e -> p v u e"),
-                picked[g][:, :, 2, lo:hi].rearrange("p u v e -> p v u e"),
+                partial[g][:, u, h_lo:h_hi],
+                picked[g][:, u, h_lo:h_hi, 0:HALF],
+                picked[g][:, u, 2 + h_lo : 2 + h_hi, 0:HALF],
                 ADD,
             )
 
-        def quantize_x(g, lo, hi):
-            nc.vector.quantize_mx(
-                out=x_codes[g][:, lo:hi].bitcast(FP8X4),
-                scales=x_scales[g][:, lo:hi],
-                in_=x_bf[g][:, lo:hi].rearrange("p v u e -> p (v u e)"),
+        def add_last(g, h, x_bf, engine):
+            engine.tensor_tensor(
+                x_bf.rearrange("p (h v u e) -> p h v u e", h=2, u=PAIRS, e=2)[:, h],
+                partial[g][:, :, h].rearrange("p u v e -> p v u e"),
+                picked[g][:, :, 4 + h, 0:HALF].rearrange("p u v e -> p v u e"),
+                ADD,
             )
 
         def interleave_w(g):
-            nc.scalar.copy(w_bf[g], w_raw[g][:].rearrange("p j n -> p n j"))
-
-        def quantize_w(g):
-            nc.vector.quantize_mx(
-                out=w_codes[g].bitcast(FP8X4),
-                scales=w_scales[g],
-                in_=w_bf[g].rearrange("p n j -> p (n j)"),
+            nc.scalar.copy(
+                w_bf[g].rearrange("p (c i j) -> p c j i", i=4, j=PACK),
+                w_raw[g][:].rearrange("p j (c i) -> p c j i", i=4),
             )
 
-        def multiply(g, h):
+        def quantize(codes, scales, values):
+            nc.vector.quantize_mx(out=codes.bitcast(FP8X4), scales=scales, in_=values)
+
+        def multiply(g, h, x_codes, x_scales, w_codes, w_scales):
             ids = slice(h * HALF, (h + 1) * HALF)
             for b in range(2):
                 rows = slice(b * P, (b + 1) * P)
                 nc.tensor.matmul_mx(
                     out=acc[h, b][:],
-                    lhsT=w_codes[g][:, rows].bitcast(FP8X4),
-                    lhsT_scale=w_scales[g][:, rows],
-                    rhs=x_codes[g][:, ids].bitcast(FP8X4),
-                    rhs_scale=x_scales[g][:, ids],
+                    lhsT=w_codes[:, rows].bitcast(FP8X4),
+                    lhsT_scale=w_scales[:, rows],
+                    rhs=x_codes[:, ids].bitcast(FP8X4),
+                    rhs_scale=x_scales[:, ids],
                     start=(g == 0),
                     stop=(g == PASSES - 1),
                 )
 
         pair_up(0)
-        gather(0, 0, 3)
-        add_first(0, nc.vector)
+        gather(0, 0)
+        gather(0, 1)
+        add_first(0, 0, 2, nc.gpsimd)
         pair_up(1)
-        gather(1, 0, 3)
-        add_first(1, nc.vector)
-        add_last(0, 0, HALF, nc.gpsimd)
-        add_last(0, HALF, V, nc.gpsimd)
+        gather(1, 0)
+        add_first(1, 0, 1, nc.gpsimd)
+        gather(1, 1)
+        add_first(1, 1, 2, nc.gpsimd)
+        add_last(0, 0, both_bf[:, 0], nc.gpsimd)
+        add_last(0, 1, both_bf[:, 0], nc.gpsimd)
         pair_up(2)
-        gather(2, 0, 3)
-        add_first(2, nc.gpsimd)
+        gather(2, 0)
+        gather(2, 1)
+        add_first(2, 0, 2, nc.gpsimd)
         pair_up(3)
-        gather(3, 0, 3)
+        gather(3, 0)
+        gather(3, 1)
+        add_first(3, 0, 1, nc.vector)
+        add_first(3, 1, 2, nc.vector)
         interleave_w(0)
-        nc.vector.quantize_mx(
-            out=both_codes[:].rearrange("p s v -> p (s v)").bitcast(FP8X4),
-            scales=both_scales[:].rearrange("p s v -> p (s v)"),
-            in_=both_bf[:].rearrange("p s c -> p (s c)"),
+        quantize(
+            both_codes[:].rearrange("p s v -> p (s v)"),
+            both_scales[:].rearrange("p s v -> p (s v)"),
+            both_bf[:].rearrange("p s c -> p (s c)"),
         )
-        multiply(0, 0)
-        multiply(0, 1)
-        add_first(3, nc.vector)
-        interleave_w(1)
-        quantize_w(1)
-        add_last(1, 0, HALF, nc.vector)
-        add_last(1, HALF, V, nc.vector)
         for h in range(2):
-            quantize_x(1, h * HALF, (h + 1) * HALF)
-            multiply(1, h)
+            multiply(0, h, both_codes[:, 0], both_scales[:, 0], both_codes[:, 1], both_scales[:, 1])
+        interleave_w(1)
+        x_bf1 = keep.tile([P, V * PACK], BF16, name="x_bf1", tag="w_raw0", align_bytes=64)
+        add_last(1, 0, x_bf1[:], nc.vector)
+        add_last(1, 1, x_bf1[:], nc.vector)
+        quantize(w_codes1[:], w_scales1[:], w_bf1[:])
+        x_codes1 = keep.tile([P, V], U32, name="x_codes1", tag="w_raw1", align_bytes=64)
+        quantize(x_codes1[:, 0:HALF], x_scales1[:, 0:HALF], x_bf1[:, 0 : HALF * PACK])
+        quantize(x_codes1[:, HALF:V], x_scales1[:, HALF:V], x_bf1[:, HALF * PACK : V * PACK])
+        for h in range(2):
+            multiply(1, h, x_codes1, x_scales1, w_codes1, w_scales1)
         nc.scalar.copy(result[0][:, 0], acc[0, 0][:])
-        nc.scalar.copy(result[0][:, 1], acc[0, 1][:])
+        nc.vector.tensor_copy(result[0][:, 1], acc[0, 1][:])
         nc.sync.dma_start(out_rows[:, :, 0:HALF], result[0][:])
-        nc.vector.tensor_copy(result[1][:, 0], acc[1, 0][:])
-        nc.scalar.copy(result[1][:, 1], acc[1, 1][:])
+        nc.scalar.copy(result[1][:, 0], acc[1, 0][:])
+        nc.vector.tensor_copy(result[1][:, 1], acc[1, 1][:])
         nc.sync.dma_start(out_rows[:, :, HALF:V], result[1][:])

@@ -18,11 +18,12 @@ PACK = 4
 PASSES = K // (P * PACK)
 PAIRS = PACK // 2
 HALF = V // 2
-RUNS = 2 * D
-RUN_COLS = HALF // 16
+LIST_COLS = D * V // 16
 PAD = 8
 CHUNK = T // 2
-VECTOR_SHARE = [352,223,223,223]
+LAP = 8
+APART = 3 * CHUNK + LAP
+VECTOR_SHARE = [352, 352, 160, 127]
 
 
 def tile_picked_hash_lin_none_sub_l_kernel(tc, xT, w, offs, out):
@@ -40,31 +41,50 @@ def tile_picked_hash_lin_none_sub_l_kernel(tc, xT, w, offs, out):
         nc.vector.memset(warm_in[:], 0.0)
         nc.scalar.copy(warm_out[:], warm_in[:])
 
-        offsets = keep.tile([P, RUNS * RUN_COLS], U16, name="offsets")
+        offsets = keep.tile([P, LIST_COLS], U16, name="offsets")
+        shared0 = keep.tile([P, CHUNK + 2 * APART], F32, name="shared0")
+        shared1 = keep.tile([P, 3 * CHUNK], F32, name="shared1")
+        partial = [
+            shared0[:, CHUNK : CHUNK + 2 * APART]
+            .rearrange("p (u s) -> p u s", u=PAIRS)[:, :, 0:CHUNK]
+            .rearrange("p u (v e) -> p u v e", e=2),
+            shared1[:, 0 : 2 * CHUNK].rearrange("p (u v e) -> p u v e", u=PAIRS, e=2),
+        ]
         raw = {}
         for q in range(PASSES * PAIRS):
             g, u = divmod(q, PAIRS)
+            rows = x_rows[g, :, 2 * u : 2 * u + 2]
             for c in range(2):
-                raw[q, c] = keep.tile([P, 2, CHUNK], F32, name="raw%d_%d" % (q, c))
-                nc.sync.dma_start(raw[q, c][:], x_rows[g, :, 2 * u : 2 * u + 2, c * CHUNK : (c + 1) * CHUNK])
+                if (q, c) == (1, 1):
+                    raw[q, c] = shared0[:, 0 : 2 * CHUNK].rearrange("p (e t) -> p e t", e=2)
+                    nc.sync.dma_start(raw[q, c], rows[:, :, CHUNK:T])
+                elif (q, c) == (2, 1):
+                    lapped = shared0[:, 2 * CHUNK : 4 * CHUNK + 2 * LAP].rearrange("p (e t) -> p e t", e=2)
+                    run_on = x_rows[g].rearrange("p j t -> p (j t)")[:, CHUNK : CHUNK + 2 * T]
+                    nc.sync.dma_start(lapped, run_on.rearrange("p (e t) -> p e t", e=2)[:, :, 0 : CHUNK + LAP])
+                    raw[q, c] = lapped[:, :, 0:CHUNK]
+                else:
+                    own = keep.tile([P, 2, CHUNK], F32, name="raw%d_%d" % (q, c))
+                    raw[q, c] = own[:]
+                    nc.sync.dma_start(raw[q, c], rows[:, :, c * CHUNK : (c + 1) * CHUNK])
             if q == 0:
                 nc.sync.dma_start(offsets[:], offs)
-        w_raw = []
+        w_raw1 = keep.tile([P, PACK, N], F32, name="w_raw1", align_bytes=64)
+        w_raw = [shared1[:, CHUNK : 3 * CHUNK].rearrange("p (j n) -> p j n", j=PACK), w_raw1[:]]
         for g in range(PASSES):
-            w_raw.append(keep.tile([P, PACK, N], F32, name="w_raw%d" % g, align_bytes=64))
-            nc.sync.dma_start(w_raw[g][:], w_rows[g])
+            nc.sync.dma_start(w_raw[g], w_rows[g])
 
         table = [keep.tile([P, T, 2], BF16, name="table%d" % q) for q in range(PASSES * PAIRS)]
         picked = [
-            keep.tile([P, PAIRS, RUNS, HALF + PAD, 2], BF16, name="picked%d" % g, align_bytes=64)
+            keep.tile([P, PAIRS, D, V + PAD, 2], BF16, name="picked%d" % g, align_bytes=64)
             for g in range(PASSES)
         ]
-        partial = [keep.tile([P, PAIRS, 2, HALF, 2], F32, name="partial%d" % g) for g in range(PASSES)]
         both_bf = keep.tile([P, 2, V * PACK], BF16, name="both_bf", align_bytes=64)
         both_codes = keep.tile([P, 2, V], U32, name="both_codes", align_bytes=64)
         both_scales = keep.tile([P, 2, V], U8, name="both_scales", align_bytes=64)
         w_bf1 = keep.tile([P, N * PACK], BF16, name="w_bf1", align_bytes=64)
         w_codes1 = keep.tile([P, N], U32, name="w_codes1", align_bytes=64)
+        x_codes1 = keep.tile([P, V], U32, name="x_codes1", align_bytes=64)
         x_scales1 = keep.tile([P, V], U8, name="x_scales1", align_bytes=64)
         w_scales1 = keep.tile([P, N], U8, name="w_scales1", align_bytes=64)
         w_bf = [both_bf[:, 1], w_bf1[:]]
@@ -73,42 +93,34 @@ def tile_picked_hash_lin_none_sub_l_kernel(tc, xT, w, offs, out):
 
         def pair_up(q):
             share = VECTOR_SHARE[q]
-            first = raw[q, 0][:].rearrange("p e t -> p t e")
-            second = raw[q, 1][:].rearrange("p e t -> p t e")
+            first = raw[q, 0].rearrange("p e t -> p t e")
+            second = raw[q, 1].rearrange("p e t -> p t e")
             nc.scalar.copy(table[q][:, 0:CHUNK, :], first)
             nc.scalar.copy(table[q][:, CHUNK : T - share, :], second[:, 0 : CHUNK - share])
             nc.vector.tensor_copy(table[q][:, T - share : T, :], second[:, CHUNK - share : CHUNK])
 
-        def gather(q, part):
+        def gather(q):
             g, u = divmod(q, PAIRS)
             window = table[q][:].rearrange("p t e -> p (t e)").bitcast(U32)
-            words = picked[g][:, u].rearrange("p r v e -> p r (v e)").bitcast(U32)
-            nc.vector.tensor_copy(
-                words[:, D * part : D * (part + 1), 0:HALF],
-                window.indirect(offsets[:, D * part * RUN_COLS : D * (part + 1) * RUN_COLS]),
-            )
+            words = picked[g][:, u].rearrange("p d v e -> p d (v e)").bitcast(U32)
+            nc.vector.tensor_copy(words[:, :, 0:V], window.indirect(offsets[:]))
 
-        def add_first(q, h_lo, h_hi, engine):
+        def add_first(q, engine):
             g, u = divmod(q, PAIRS)
-            engine.tensor_tensor(
-                partial[g][:, u, h_lo:h_hi],
-                picked[g][:, u, h_lo:h_hi, 0:HALF],
-                picked[g][:, u, 2 + h_lo : 2 + h_hi, 0:HALF],
-                ADD,
-            )
+            engine.tensor_tensor(partial[g][:, u], picked[g][:, u, 0, 0:V], picked[g][:, u, 1, 0:V], ADD)
 
-        def add_last(g, h, x_bf, engine):
+        def add_last(g, lo, hi, x_bf, engine):
             engine.tensor_tensor(
-                x_bf.rearrange("p (h v u e) -> p h v u e", h=2, u=PAIRS, e=2)[:, h],
-                partial[g][:, :, h].rearrange("p u v e -> p v u e"),
-                picked[g][:, :, 4 + h, 0:HALF].rearrange("p u v e -> p v u e"),
+                x_bf.rearrange("p (v u e) -> p v u e", u=PAIRS, e=2)[:, lo:hi],
+                partial[g][:, :, lo:hi].rearrange("p u v e -> p v u e"),
+                picked[g][:, :, 2, lo:hi].rearrange("p u v e -> p v u e"),
                 ADD,
             )
 
         def interleave_w(g):
             nc.scalar.copy(
                 w_bf[g].rearrange("p (c i j) -> p c j i", i=4, j=PACK),
-                w_raw[g][:].rearrange("p j (c i) -> p c j i", i=4),
+                w_raw[g].rearrange("p j (c i) -> p c j i", i=4),
             )
 
         def quantize(codes, scales, values):
@@ -129,25 +141,17 @@ def tile_picked_hash_lin_none_sub_l_kernel(tc, xT, w, offs, out):
                 )
 
         pair_up(0)
-        gather(0, 0)
-        gather(0, 1)
-        add_first(0, 0, 2, nc.gpsimd)
+        gather(0)
         pair_up(1)
-        gather(1, 0)
-        add_first(1, 0, 1, nc.gpsimd)
-        gather(1, 1)
-        add_first(1, 1, 2, nc.gpsimd)
-        add_last(0, 0, both_bf[:, 0], nc.gpsimd)
-        add_last(0, 1, both_bf[:, 0], nc.gpsimd)
+        add_first(0, nc.gpsimd)
+        gather(1)
         pair_up(2)
-        gather(2, 0)
-        gather(2, 1)
-        add_first(2, 0, 2, nc.gpsimd)
+        add_first(1, nc.vector)
+        add_last(0, 0, V, both_bf[:, 0], nc.gpsimd)
+        gather(2)
+        add_first(2, nc.gpsimd)
         pair_up(3)
-        gather(3, 0)
-        gather(3, 1)
-        add_first(3, 0, 1, nc.vector)
-        add_first(3, 1, 2, nc.vector)
+        gather(3)
         interleave_w(0)
         quantize(
             both_codes[:].rearrange("p s v -> p (s v)"),
@@ -156,12 +160,12 @@ def tile_picked_hash_lin_none_sub_l_kernel(tc, xT, w, offs, out):
         )
         for h in range(2):
             multiply(0, h, both_codes[:, 0], both_scales[:, 0], both_codes[:, 1], both_scales[:, 1])
+        add_first(3, nc.vector)
         interleave_w(1)
-        x_bf1 = keep.tile([P, V * PACK], BF16, name="x_bf1", tag="w_raw0", align_bytes=64)
-        add_last(1, 0, x_bf1[:], nc.vector)
-        add_last(1, 1, x_bf1[:], nc.vector)
         quantize(w_codes1[:], w_scales1[:], w_bf1[:])
-        x_codes1 = keep.tile([P, V], U32, name="x_codes1", tag="w_raw1", align_bytes=64)
+        x_bf1 = keep.tile([P, V * PACK], BF16, name="x_bf1", tag="w_raw1", align_bytes=64)
+        add_last(1, 0, HALF, x_bf1[:], nc.vector)
+        add_last(1, HALF, V, x_bf1[:], nc.vector)
         quantize(x_codes1[:, 0:HALF], x_scales1[:, 0:HALF], x_bf1[:, 0 : HALF * PACK])
         quantize(x_codes1[:, HALF:V], x_scales1[:, HALF:V], x_bf1[:, HALF * PACK : V * PACK])
         for h in range(2):

from contextlib import ExitStack

import concourse.mybir as mybir

K, T, D, V, N = 1024, 1024, 3, 256, 256
FLOPS = 2 * K * N * V

F32 = mybir.dt.float32
BF16 = mybir.dt.bfloat16
U32 = mybir.dt.uint32
U16 = mybir.dt.uint16
U8 = mybir.dt.uint8
FP8X4 = mybir.dt.float8_e4m3fn_x4
ADD = mybir.AluOpType.add

P = 128
PACK = 4
PASSES = K // (P * PACK)
PAIRS = PACK // 2
HALF = V // 2
LIST_COLS = D * V // 16
PAD = 8
CHUNK = T // 2
LAP = 8
APART = 3 * CHUNK + LAP
VECTOR_SHARE = [352, 352, 160, 127]


def tile_picked_hash_lin_none_sub_l_kernel(tc, xT, w, offs, out):
    nc = tc.nc
    x_rows = xT.rearrange("(g p j) t -> g p j t", p=P, j=PACK)
    w_rows = w.rearrange("(g p j) n -> g p j n", p=P, j=PACK)
    out_rows = out.rearrange("(b p) v -> p b v", p=P)

    with ExitStack() as ctx:
        keep = ctx.enter_context(tc.tile_pool(name="keep", bufs=1))
        psum = ctx.enter_context(tc.psum_pool(name="psum", bufs=1))

        warm_in = keep.tile([P, 8], F32, name="warm_in")
        warm_out = keep.tile([P, 8], BF16, name="warm_out")
        nc.vector.memset(warm_in[:], 0.0)
        nc.scalar.copy(warm_out[:], warm_in[:])

        offsets = keep.tile([P, LIST_COLS], U16, name="offsets")
        shared0 = keep.tile([P, CHUNK + 2 * APART], F32, name="shared0")
        shared1 = keep.tile([P, 3 * CHUNK], F32, name="shared1")
        partial = [
            shared0[:, CHUNK : CHUNK + 2 * APART]
            .rearrange("p (u s) -> p u s", u=PAIRS)[:, :, 0:CHUNK]
            .rearrange("p u (v e) -> p u v e", e=2),
            shared1[:, 0 : 2 * CHUNK].rearrange("p (u v e) -> p u v e", u=PAIRS, e=2),
        ]
        raw = {}
        for q in range(PASSES * PAIRS):
            g, u = divmod(q, PAIRS)
            rows = x_rows[g, :, 2 * u : 2 * u + 2]
            for c in range(2):
                if (q, c) == (1, 1):
                    raw[q, c] = shared0[:, 0 : 2 * CHUNK].rearrange("p (e t) -> p e t", e=2)
                    nc.sync.dma_start(raw[q, c], rows[:, :, CHUNK:T])
                elif (q, c) == (2, 1):
                    lapped = shared0[:, 2 * CHUNK : 4 * CHUNK + 2 * LAP].rearrange("p (e t) -> p e t", e=2)
                    run_on = x_rows[g].rearrange("p j t -> p (j t)")[:, CHUNK : CHUNK + 2 * T]
                    nc.sync.dma_start(lapped, run_on.rearrange("p (e t) -> p e t", e=2)[:, :, 0 : CHUNK + LAP])
                    raw[q, c] = lapped[:, :, 0:CHUNK]
                else:
                    own = keep.tile([P, 2, CHUNK], F32, name="raw%d_%d" % (q, c))
                    raw[q, c] = own[:]
                    nc.sync.dma_start(raw[q, c], rows[:, :, c * CHUNK : (c + 1) * CHUNK])
            if q == 0:
                nc.sync.dma_start(offsets[:], offs)
        w_raw1 = keep.tile([P, PACK, N], F32, name="w_raw1", align_bytes=64)
        w_raw = [shared1[:, CHUNK : 3 * CHUNK].rearrange("p (j n) -> p j n", j=PACK), w_raw1[:]]
        for g in range(PASSES):
            nc.sync.dma_start(w_raw[g], w_rows[g])

        table = [keep.tile([P, T, 2], BF16, name="table%d" % q) for q in range(PASSES * PAIRS)]
        picked = [
            keep.tile([P, PAIRS, D, V + PAD, 2], BF16, name="picked%d" % g, align_bytes=64)
            for g in range(PASSES)
        ]
        both_bf = keep.tile([P, 2, V * PACK], BF16, name="both_bf", align_bytes=64)
        both_codes = keep.tile([P, 2, V], U32, name="both_codes", align_bytes=64)
        both_scales = keep.tile([P, 2, V], U8, name="both_scales", align_bytes=64)
        w_bf1 = keep.tile([P, N * PACK], BF16, name="w_bf1", align_bytes=64)
        w_codes1 = keep.tile([P, N], U32, name="w_codes1", align_bytes=64)
        x_codes1 = keep.tile([P, V], U32, name="x_codes1", align_bytes=64)
        x_scales1 = keep.tile([P, V], U8, name="x_scales1", align_bytes=64)
        w_scales1 = keep.tile([P, N], U8, name="w_scales1", align_bytes=64)
        w_bf = [both_bf[:, 1], w_bf1[:]]
        acc = {(h, b): psum.tile([P, HALF], F32, name="acc%d_%d" % (h, b)) for h in range(2) for b in range(2)}
        result = [keep.tile([P, 2, HALF], F32, name="result%d" % h) for h in range(2)]

        def pair_up(q):
            share = VECTOR_SHARE[q]
            first = raw[q, 0].rearrange("p e t -> p t e")
            second = raw[q, 1].rearrange("p e t -> p t e")
            nc.scalar.copy(table[q][:, 0:CHUNK, :], first)
            nc.scalar.copy(table[q][:, CHUNK : T - share, :], second[:, 0 : CHUNK - share])
            nc.vector.tensor_copy(table[q][:, T - share : T, :], second[:, CHUNK - share : CHUNK])

        def gather(q):
            g, u = divmod(q, PAIRS)
            window = table[q][:].rearrange("p t e -> p (t e)").bitcast(U32)
            words = picked[g][:, u].rearrange("p d v e -> p d (v e)").bitcast(U32)
            nc.vector.tensor_copy(words[:, :, 0:V], window.indirect(offsets[:]))

        def add_first(q, engine):
            g, u = divmod(q, PAIRS)
            engine.tensor_tensor(partial[g][:, u], picked[g][:, u, 0, 0:V], picked[g][:, u, 1, 0:V], ADD)

        def add_last(g, lo, hi, x_bf, engine):
            engine.tensor_tensor(
                x_bf.rearrange("p (v u e) -> p v u e", u=PAIRS, e=2)[:, lo:hi],
                partial[g][:, :, lo:hi].rearrange("p u v e -> p v u e"),
                picked[g][:, :, 2, lo:hi].rearrange("p u v e -> p v u e"),
                ADD,
            )

        def interleave_w(g):
            nc.scalar.copy(
                w_bf[g].rearrange("p (c i j) -> p c j i", i=4, j=PACK),
                w_raw[g].rearrange("p j (c i) -> p c j i", i=4),
            )

        def quantize(codes, scales, values):
            nc.vector.quantize_mx(out=codes.bitcast(FP8X4), scales=scales, in_=values)

        def multiply(g, h, x_codes, x_scales, w_codes, w_scales):
            ids = slice(h * HALF, (h + 1) * HALF)
            for b in range(2):
                rows = slice(b * P, (b + 1) * P)
                nc.tensor.matmul_mx(
                    out=acc[h, b][:],
                    lhsT=w_codes[:, rows].bitcast(FP8X4),
                    lhsT_scale=w_scales[:, rows],
                    rhs=x_codes[:, ids].bitcast(FP8X4),
                    rhs_scale=x_scales[:, ids],
                    start=(g == 0),
                    stop=(g == PASSES - 1),
                )

        pair_up(0)
        gather(0)
        pair_up(1)
        add_first(0, nc.gpsimd)
        gather(1)
        pair_up(2)
        add_first(1, nc.vector)
        add_last(0, 0, V, both_bf[:, 0], nc.gpsimd)
        gather(2)
        add_first(2, nc.gpsimd)
        pair_up(3)
        gather(3)
        interleave_w(0)
        quantize(
            both_codes[:].rearrange("p s v -> p (s v)"),
            both_scales[:].rearrange("p s v -> p (s v)"),
            both_bf[:].rearrange("p s c -> p (s c)"),
        )
        for h in range(2):
            multiply(0, h, both_codes[:, 0], both_scales[:, 0], both_codes[:, 1], both_scales[:, 1])
        add_first(3, nc.vector)
        interleave_w(1)
        quantize(w_codes1[:], w_scales1[:], w_bf1[:])
        x_bf1 = keep.tile([P, V * PACK], BF16, name="x_bf1", tag="w_raw1", align_bytes=64)
        add_last(1, 0, HALF, x_bf1[:], nc.vector)
        add_last(1, HALF, V, x_bf1[:], nc.vector)
        quantize(x_codes1[:, 0:HALF], x_scales1[:, 0:HALF], x_bf1[:, 0 : HALF * PACK])
        quantize(x_codes1[:, HALF:V], x_scales1[:, HALF:V], x_bf1[:, HALF * PACK : V * PACK])
        for h in range(2):
            multiply(1, h, x_codes1, x_scales1, w_codes1, w_scales1)
        nc.scalar.copy(result[0][:, 0], acc[0, 0][:])
        nc.vector.tensor_copy(result[0][:, 1], acc[0, 1][:])
        nc.sync.dma_start(out_rows[:, :, 0:HALF], result[0][:])
        nc.scalar.copy(result[1][:, 0], acc[1, 0][:])
        nc.vector.tensor_copy(result[1][:, 1], acc[1, 1][:])
        nc.sync.dma_start(out_rows[:, :, HALF:V], result[1][:])
